import numpy as np, ml_dtypes
CORES = [16,17,18,19,32,33,34,35]
N = 8
BF = ml_dtypes.bfloat16
W, K, LP, CAP, PR = 4096, 4096, 1, 512, 5
XS = (1, 2, 4)
MP = K >> LP
def coefs(rng, lo, hi):
    o = np.argsort(rng.random((8, 16, 16)), axis=1)
    v = rng.integers(1, 4, (8, 16, 16)) * np.where(o == 0, 1, np.where(o == 1, -1, 2 * rng.integers(0, 2, (8, 16, 16)) - 1))
    return np.where(o < rng.integers(lo, hi + 1, (8, 1, 16)), v, 0)
def rays(rng, top, dens):
    v = np.floor(rng.random((N, 8, 16, W)) * (np.reshape(top, (1, 8, 1, 1)) + 1.0))
    return (v * (rng.random((N, 8, 16, W)) < dens)).astype(np.int64)
def plant(rng, nn, pz, order, full=False, odd=()):
    c = coefs(rng, 6, 10); x = rng.integers(0, 16, (N, 8, 16, W))
    P = np.argsort(rng.random((8, 16)), axis=1); M = rng.integers(0, 16, 8)
    if full: x[:, 1::2] = np.floor(np.exp2(7.9 * rng.random((N, 4, 16, W)))).astype(np.int64)
    for g in range(8):
        m = M[g]; a, b, e = P[g, :3]; w = int(rng.integers(1, 4))
        if full or g in odd:
            c[g] = 2 * np.sign(c[g]); c[g, e] = rng.choice(np.array([-3, -1, 1, 3]), 16); x[:, g, e] |= 1
        c[g, :, m] = 0; c[g, a, m] = w; c[g, b, m] = -w
        for r in range(N):
            sg = np.zeros(W, np.int64); sg[:int(nn[r, g])] = -1; sg[W - int(pz[r, g]):] = 1
            if order[g] == 0: sg = rng.permutation(sg)
            if order[g] == 2: sg = sg[::-1]
            lo = rng.integers(0, 8, W); d = rng.integers(1, 8, W)
            if full: d = np.where(sg > 0, 7, 1)
            x[r, g, a] = lo + np.where(sg > 0, d, 0); x[r, g, b] = lo + np.where(sg < 0, d, 0)
    return x, c, P, M
def pack(x, c):
    return {"x": np.ascontiguousarray(x.reshape(N, 128, W)).astype(np.float32).astype(BF), "q": np.stack([c.reshape(128, 16)] * N).astype(np.int32)}
def setup_inputs(rng):
    top = rng.permutation(np.array([15, 15, 40, 40, 100, 100, 255, 255]))
    return pack(rays(rng, top, rng.choice(np.array([0.1, 0.3, 0.6, 1.0]), (N, 8, 16, 1))), coefs(rng, 2, 6))
def setup_inputs_room(rng):
    nn = rng.choice(np.array([0, 1, CAP - 1, CAP, CAP + 1, 2 * CAP]), (N, 8)); pz = rng.choice(np.array([0, 1, MP - 1, MP, MP + 1]), (N, 8))
    nn[0] = (CAP, CAP + 1, CAP - 1, CAP, 1, 0, 2 * CAP, CAP + 1); pz[0] = (MP, MP + 1, MP - 1, 1, MP, MP + 1, MP, 0)
    nn[XS[0]] = (2 * CAP, CAP, CAP + 1, CAP - 1, CAP, CAP, 1, CAP); pz[XS[0]] = (MP + 1, MP, MP, MP - 1, MP, MP + 1, MP, MP)
    x, c, P, M = plant(rng, nn, pz, np.zeros(8, np.int64))
    return pack(x, c)
def setup_inputs_full(rng):
    few = CAP + rng.integers(0, 64, (N, 8)); many = W - MP - rng.integers(72, 136, (N, 8))
    nn = np.where(np.array([0, 1, 1, 0, 0, 1, 1, 0]) == 1, many, few); pz = MP + rng.integers(0, 64, (N, 8))
    o = XS[0]; p = W // (2 ** LP + 1)
    nn[0, 0] = CAP; nn[o, 3] = CAP; pz[0, :2] = MP; nn[0, 2] = W - p; pz[0, 2] = p
    x, c, P, M = plant(rng, nn, pz, np.array([0, 0, 0, 0, 1, 1, 2, 2]), True)
    a, b, e, f0, f1, f2, f3 = P[2, :7]
    up = x[0, 2, a] > x[0, 2, b]; dn = x[o, 2, a] < x[o, 2, b]
    x[0, 2, a] = np.where(up, rng.integers(1, 16, W), 0); x[0, 2, b] = np.where(up, 0, rng.integers(2, 8, W))
    u = np.zeros(W, np.int64); u[up] = rng.permutation(4096)[:p]
    for k, v in ((f0, u >> 6), (f1, 63 - (u >> 6)), (f2, u & 63), (f3, 63 - (u & 63))):
        x[0, 2, k] = np.where(up, v, x[0, 2, k]); x[o, 2, k] = np.where(dn, 0, x[o, 2, k])
    x[o, 2, a] = np.where(dn, 0, x[o, 2, a]); x[o, 2, b] = np.where(dn, 1, x[o, 2, b])
    return pack(x, c)
def setup_inputs_ties(rng):
    c = coefs(rng, 2, 4); c[:, :, 8:] = -c[:, :, rng.permutation(8)]; c[0, :, 15] = 0; c[4, :, 0] = 0
    x = rays(rng, np.array([1, 1, 2, 2, 3, 1, 2, 15]), rng.choice(np.array([0.4, 0.6, 0.9]), (N, 8, 16, 1)))
    h = W // 2
    for g in (2, 5): x[:, g, :, h:] = x[:, g][:, :, rng.permutation(h)]
    x[:, 7] = 255 * (rng.random((N, 16, W)) < 0.4)
    return pack(x, c)
def setup_inputs_lean(rng):
    h = W // 2; nn = rng.integers(h // 4, h // 2, (N, 8)); pz = rng.integers(h // 4, h // 2, (N, 8)); o = XS[0]
    nn[:, 0] = 0; pz[:, 1] = 0
    nn[0, 2] = W; pz[0, 2] = 0; nn[o, 2] = h; pz[o, 2] = W - h
    nn[0, 3] = 0; pz[0, 3] = 0; nn[o, 3] = 0; pz[o, 3] = W
    nn[0, 6] = 1; pz[0, 6] = W - 1
    for r in (0, XS[1], XS[0] ^ XS[1]): nn[r, 4] = h // 2; pz[r, 4] = h // 16
    nn[o, 4] = 16; pz[o, 4] = h // 2
    x, c, P, M = plant(rng, nn, pz, np.array([0, 0, 0, 0, 1, 2, 1, 2]), False, (0, 1, 4))
    a, b, e, k, l = P[0, :5]; m = M[0]
    c[0][:, [0, m]] = c[0][:, [m, 0]]; c[0, b, 0] = 0; x[:, 0, a] -= x[:, 0, b]
    c[0, :, 1] = 0; c[0, e, 1] = 2 * rng.integers(0, 2) - 1; c[0, k, 1] = 2; c[0, l, 1] = -2
    a, b = P[1, :2]; c[1, a, M[1]] = 0; x[:, 1, b] -= x[:, 1, a]
    c[4, :, (M[4] + rng.integers(1, 16)) % 16] = c[4, :, M[4]]
    return pack(x, c)
def setup_inputs_spread(rng):
    u = rng.random((N, 8, 16, W)); u[:, 6] = 0.5 + 0.5 * u[:, 6]
    v = np.floor(np.exp2(3 + 5 * rng.random((N, 8, 1, W))) * u) * (rng.random((N, 8, 1, W)) > 0.0625)
    kept = rng.random((N, 8, 16, W)) < rng.choice(np.array([0.4, 0.7, 1.0]), (N, 8, 16, 1)); kept[:, 6] = True
    v = np.minimum(v * kept, 255).astype(np.int64); c = coefs(rng, 2, 16)
    up = rng.permutation(16) < 8; side = (rng.random((N, 1, W)) < 0.5) == up[None, :, None]
    v[:, 7] = np.where(side, rng.integers(192, 256, (N, 16, W)), rng.integers(0, 32, (N, 16, W)))
    c[7] = np.where(up[:, None], 1, -1) * rng.choice(np.array([2, 3, 3, 3]), (16, 16)) * rng.choice(np.array([-1, 1]), (1, 16))
    return pack(v, c)
def check_inputs(d):
    bad = []; x = np.asarray(d["x"]).astype(np.float32); q = np.asarray(d["q"])
    if not (np.all(x >= 0) and np.all(x <= 255) and np.all(x == np.floor(x))): bad.append("range of x")
    if np.min(q) < -3 or np.max(q) > 3: bad.append("range of q")
    if not np.all(q == q[:1]): bad.append("q alike on all ranks")
    return bad
def reference(x, q):
    cur = np.ascontiguousarray(x.astype(np.float32).reshape(N, 8, 16, W).transpose(0, 1, 3, 2)).astype(np.int16)
    co = q[0].astype(np.float32).reshape(8, 16, 16)
    used = np.zeros((8, 16), bool)
    k = np.arange(K); i = k >> LP
    for t in range(len(XS)):
        val = np.matmul(cur.astype(np.float32), co[None])
        cnt = np.where(used, N * W + 1, np.count_nonzero(val, axis=(0, 2)))
        m = np.argmin(cnt, axis=1)
        used[np.arange(8), m] = True
        s = np.take_along_axis(val, m[None, :, None, None], 3)[..., 0].astype(np.int64)
        j = (37 * i + (CAP >> LP) * (k & (2 ** LP - 1)) + t) & (CAP - 1)
        new = cur.copy()
        for r in range(N):
            o = r ^ XS[t]
            for g in range(8):
                own = cur[r, g]; neg = np.flatnonzero(s[r, g] < 0); pos = np.flatnonzero(s[r, g] > 0); guest = np.flatnonzero(s[o, g] < 0)[:CAP]
                ks = np.flatnonzero((i < len(pos)) & (j < len(guest)))
                a = pos[i[ks]]; b = guest[j[ks]]; keep = s[r, g, a] + s[o, g, b] >= 0
                a = a[keep]; b = b[keep]
                z = np.minimum(own[a] + cur[o, g][b], 255)
                v = (17 * a + 5 * j[ks][keep]) & (W - 1); alive = np.ones(len(a), bool)
                for n in range(PR):
                    c = np.where(v == a, 16, np.count_nonzero(own[v] > z, axis=1))
                    alive = alive & (c > 0)
                    v = (5 * v + 241 * c + 1) & (W - 1)
                z = z[alive]; h = min(len(z), len(neg))
                new[r, g, neg[:h]] = z[:h]
        cur = new
    return {"y": np.ascontiguousarray(cur.transpose(0, 1, 3, 2)).reshape(N, 128, W).astype(np.float32).astype(BF)}

from concourse.bass import DstId, RemoteDMATransfer
from concourse.mybir import AluOpType as O, AxisListType as AX, ActivationFunctionType as AF

W, ZC, ZW, FW, GW = 4096, 2736, 2816, 288, 576
XS = (1, 2, 4)
NA = 896
BF, F32, I32, U16 = "bfloat16", "float32", "int32", "uint16"
_S = {
    "xa": (W + ZW, BF), "xb": (W + ZW, BF), "xc": (W, BF), "z": (W + 16, BF), "msk": (W, BF), "st": (W, BF), "nz": (W, BF), "pp": (2048, BF),
    "ga": (2048, BF), "tab": (5920, BF), "ld": (23 * 128, BF), "g1": (512, BF), "ft": (256, BF), "fl": (2 * FW, BF), "gx": (2 * FW + 16, BF),
    "keep": (2 * FW, BF), "hi": (2 * 560, BF), "d1": (544, BF), "sc": (544, F32), "n8": (544, BF), "lwp": (816, F32), "lwn": (816, F32),
    "lws": (816, F32), "b8": (272, F32), "ik": (256, F32), "j5": (128, F32), "jk": (64, F32), "pj": (32, U16), "jb": (160, I32),
    "j0": (144, F32), "jr": (144, BF), "tf": (256, F32), "tf2": (256, F32), "ti": (256, I32), "ti2": (256, I32), "tb": (256, BF), "eh": (256, BF),
    "col": (40, F32), "ci": (8, I32), "qi": (16, I32), "qf": (16, F32), "qbd": (128, BF), "idn": (136, BF), "nid": (128, BF), "i38": (128, BF),
    "bo": (128, BF), "bof": (128, F32), "one": (128, BF), "tri": (128, BF), "rt": (128, BF), "wc": (144, BF), "w1": (144, BF), "w2": (144, BF),
    "w256": (144, BF), "a1": (144, BF), "a2": (144, BF), "wq": (144, BF), "wq2": (144, BF), "og": (32, F32), "kr": (32, F32), "r2": (16, BF),
    "rowc": (16, BF), "s16": (36, BF), "dmp": (36, F32), "pm": (512, F32), "osel": (16, U16), "olo": (72, U16), "ohi": (72, U16),
    "osc": (36, U16), "ol": (256, U16), "op": (128, U16), "off": (256, U16), "w": (256, F32), "v": (256, I32), "t": (256, I32), "eq": (256, BF),
    "al": (6 * 256, BF), "alv": (256, BF), "nsg": (64, F32), "c01": (72, I32), "kp": (256, BF), "kt": (256, BF), "dg": (136, F32),
    "nw": (256, F32), "lo": (544, BF), "b9": (272, F32), "cnt0": (36, F32), "cnt1": (36, F32), "cnt2": (36, F32),
    "gs0": (GW, BF), "gs1": (GW, BF), "gs2": (GW, BF), "gl0": (GW, BF), "gl1": (GW, BF), "gl2": (GW, BF),
}
SCRATCH = {n: ("sbuf", [128, w], d) for n, (w, d) in _S.items()}
SCRATCH.update({"p%d" % i: ("psum", [128, 512], F32) for i in range(8)})
SEMAPHORES = ["ev", "ea", "ep", "eg", "lq", "lx0", "lx1", "sty", "sent", "cn0", "cn1", "cn2", "gu0", "gu1", "gu2"]


def _emit(g, T, ops, final):
    qs = {"v": g.vector, "a": g.scalar, "p": g.tensor, "g": g, "s": g.sync}
    hist, clock, snap, need, sig = {}, {e: {} for e in qs}, [], [], set()
    for i, o in enumerate(ops):
        e, deps = o["e"], set()
        for kind, regs in (("r", o["r"]), ("w", o["w"])):
            for n, a, b, s in regs:
                bank = n[0] == "p" and n[1:].isdigit()
                for k2, a2, b2, s2, j in hist.get(n, ()):
                    same = ops[j]["e"] == e and not ops[j]["tok"] and not o["tok"]
                    if bank and not same:
                        deps.add(j)
                    elif (a < b2 and a2 < b and (kind, k2) != ("r", "r") and not (same and e == "p")
                          and not (s == s2 > 1 and (a - a2) % s)):
                        deps.add(j)
        for kind, regs in (("r", o["r"]), ("w", o["w"])):
            for n, a, b, s in regs:
                h = hist.setdefault(n, [])
                if kind == "w" and s == 1:
                    h[:] = [x for x in h if not (a <= x[1] and x[2] <= b)]
                h.append((kind, a, b, s, i))
        if e is None:
            snap.append({}); need.append([]); continue
        ck, ws = clock[e], []
        for j in sorted(deps, reverse=True):
            key = ops[j]["tok"][0] if ops[j]["tok"] else ops[j]["e"]
            if ck.get(key, -1) >= j:
                continue
            ws.append(j); sig.add(j); ck[key] = j
            for k, val in snap[j].items():
                if ck.get(k, -1) < val:
                    ck[k] = val
        snap.append(dict(ck)); need.append(ws)
    cnt, val = {e: 0 for e in "vapg"}, {}
    for i, o in enumerate(ops):
        if o["tok"]:
            val[i] = o["tok"]
        elif i in sig:
            cnt[o["e"]] += 1; val[i] = ("e" + o["e"], cnt[o["e"]])
    for i, o in enumerate(ops):
        if o["e"] is None:
            continue
        q = qs[o["e"]]
        for j in need[i]:
            q.wait_ge(T.sem[val[j][0]], val[j][1])
        ins = o["f"](q)
        if o["dma"]:
            ins.then_inc(T.sem[o["dma"]], 16)
        elif i in sig and not o["tok"]:
            ins.then_inc(T.sem[val[i][0]], 1)
    for e in "vapg":
        if cnt[e]:
            g.wait_ge(T.sem["e" + e], cnt[e])
    for s, n in final:
        g.wait_ge(T.sem[s], n)


def rank_program(g, core, T, topo):
    rank = T.rank_of(core)
    if rank is None:
        return
    cores = list(T.cores)
    ops, sent = [], [0]

    def A(n, a=0, b=None, s=1):
        b = T[n].shape[1] if b is None else b
        return (T[n][:, a:b] if s == 1 else T[n][:, a:b:s], [(n, a, b, s)], [])

    def C(i):
        return A("col", i, i + 1)

    def PB(i, a=0, b=512, s=1):
        return A("p%d" % i, a, b, s)

    def IND(win, off):
        return (win[0].indirect(off[0]), win[1], off[1])

    def rec(e, f, out, ins, tok=None, dma=None):
        r = list(out[2]) if out else []
        for x in ins:
            if isinstance(x, tuple):
                r += x[1] + x[2]
        ops.append({"e": e, "f": f, "w": out[1] if out else [], "r": r, "tok": tok, "dma": dma})

    def ap(x):
        return x[0] if isinstance(x, tuple) else x

    def tt(o, a, b, op):
        rec("v", lambda q: q.tensor_tensor(o[0], a[0], b[0], op), o, [a, b])

    def ts(o, a, s1, op0, s2=None, op1=None):
        if op1 is None:
            rec("v", lambda q: q.tensor_scalar(o[0], a[0], ap(s1), None, op0), o, [a, s1])
        else:
            rec("v", lambda q: q.tensor_scalar(o[0], a[0], ap(s1), ap(s2), op0, op1), o, [a, s1, s2])

    def cp(o, a):
        rec("v", lambda q: q.tensor_copy(o[0], a[0]), o, [a])

    def ms(o, c):
        rec("v", lambda q: q.memset(o[0], c), o, [])

    def red(o, a, op):
        rec("v", lambda q: q.tensor_reduce(o[0], a[0], AX.X, op), o, [a])

    def scan(o, d0, d1, ini, op0, op1):
        rec("v", lambda q: q.tensor_tensor_scan(o[0], d0[0], d1[0], ap(ini), op0, op1), o, [d0, d1, ini])

    def act(o, a, fn=AF.Identity, bias=0.0, scale=1.0):
        rec("a", lambda q: q.activation(o[0], a[0], fn, bias=ap(bias), scale=ap(scale)), o, [a, bias, scale])

    def mm1(o, l, r, start, stop):
        rec("p", lambda q: q.matmul(o[0], l[0], r[0], start, stop), o, [l, r])

    def mm(o, terms):
        for i, (l, r) in enumerate(terms):
            mm1(o, l, r, i == 0, i == len(terms) - 1)

    def iota(o, pat, base=0, cm=0, isint=False):
        if isint:
            rec("g", lambda q: q.iota(o[0], pat, base, cm), o, [])
        else:
            rec("g", lambda q: q.iota(o[0], pat, base, cm, allow_small_or_imprecise_dtypes=True), o, [])

    def fill(n, a, b, c):
        iota(A(n, a, b), [[0, b - a]], c)

    def win(n, c):
        return A(n, 15 - c, 143 - c)

    IDN = A("idn", 0, 128)

    rec("a", lambda q: q.dma_start(T.qi[:], T.q[:]), A("qi"), [], ("lq", 16), "lq")
    for h in range(2):
        rec("s", lambda q, h=h: q.dma_start(T.xa[:, 2048 * h:2048 * h + 2048], T.x[:, 2048 * h:2048 * h + 2048]),
            A("xa", 2048 * h, 2048 * h + 2048), [], ("lx%d" % h, 16), "lx%d" % h)

    def consts_a():
        iota(A("ci", 0, 1), [[0, 1]], 0, 1, True)
        iota(A("og", 16, 32), [[0, 2], [1, 8]])
        iota(A("j0"), [[1, 144]])
        iota(A("tf"), [[1, 256]])
        iota(A("tb", 0, 128), [[0, 16], [1, 8]])
        iota(A("rt"), [[0, 8], [1, 16]])
        iota(A("bof"), [[1, 8], [0, 16]])
        iota(A("rowc"), [[128, 2], [1, 8]])
        fill("one", 0, 128, 1)
        iota(A("jb", 0, 128), [[296, 128]], 0, 0, True)
        iota(A("jb", 128, 160), [[592, 32]], 0, 0, True)
        iota(A("dmp"), [[0, 2], [16, 18]], 272, 0)
        iota(A("b8"), [[16, 272]], 8)
        for c, (s1, s2) in {1: (4, 7), 2: (0, 15), 3: (0, 1), 4: (0, 7), 5: (3, 7), 6: (3, 1), 7: (1, 7)}.items():
            ts(A("ci", c, c + 1), A("ci", 0, 1), s1, O.logical_shift_right, s2, O.bitwise_and)
        cp(A("col", 0, 8), A("ci"))
        ts(A("og", 16, 32), A("og", 16, 32), C(1), O.is_equal)
        ts(C(8), C(1), 16.0, O.mult)
        ts(C(11), C(2), -256.0, O.mult, -128.0, O.add)
        ts(A("jr"), A("j0"), C(8), O.subtract)
        act(A("tri"), A("jr", 0, 128), AF.Sigmoid, bias=C(11), scale=256.0)
        cp(A("qf"), A("qi"))
        for k in range(8):
            act(A("qbd", 16 * k, 16 * k + 16), A("qf"), scale=A("og", 16 + k, 17 + k))
        ms(A("kr", 0, 8), 2.0); ms(A("kr", 8, 16), 0.0)
        ts(A("kr", 24, 32), A("j0", 0, 8), C(4), O.is_equal)
        scan(A("kr", 16, 24), A("kr", 0, 8), A("kr", 8, 16), 0.5, O.mult, O.add)
        tt(A("kr", 24, 32), A("kr", 24, 32), A("kr", 16, 24), O.mult)
        red(C(9), A("kr", 24, 32), O.add)
        rec("v", lambda q: q.reciprocal(C(10)[0], C(9)[0]), C(10), [C(9)])
        ts(A("tb", 128, 256), A("tb", 0, 128), C(0), O.is_gt)
        ts(A("ti"), A("tf"), C(10), O.mult, -0.496, O.add)
        ts(C(12), C(0), 64.0, O.is_ge, 8192.0, O.mult)
        ts(A("ti2"), A("ti"), 1, O.bitwise_and)
        ts(C(12), C(12), C(4), O.max)
        cp(A("eh"), A("ti2"))
        ts(A("rt"), A("rt"), C(5), O.subtract)
        mm(PB(7, 0, 256), [(A("tb", 128, 256), A("eh"))])
        ts(IDN, A("jr", 0, 128), C(2), O.is_equal)
        ts(A("tb"), PB(7, 0, 256), C(5), O.is_equal)
        tt(A("eh"), A("eh"), A("tb"), O.mult)
        for d in range(23):
            ts(A("ld", 128 * d, 128 * d + 128), A("rt"), float(d - 7), O.is_equal, C(12), O.mult)
        act(A("idn", 128, 136), A("og", 16, 24))
        act(A("rowc"), A("rowc"), scale=0.125)
        act(C(26), C(2), scale=128.0)
        act(A("cnt0", 32, 33), C(2), scale=0.0625, bias=0.0625)

    def table(k, bk):
        n = min(2, 23 - 2 * k)
        for d in range(n):
            mm(PB(bk, 256 * d, 256 * d + 256), [(A("ld", 128 * (2 * k + d), 128 * (2 * k + d + 1)), A("eh"))])
        act(A("tab", 16 + 512 * k, 16 + 512 * k + 256 * n), PB(bk, 0, 256 * n), bias=-8192.0)

    def consts_b():
        fill("fl", 256, FW, 0); fill("fl", FW + 256, 2 * FW, 0); fill("keep", 0, 2 * FW, 1); fill("keep", FW - 1, FW, 0); fill("gx", 0, 1, 0)
        fill("s16", 0, 36, 0)
        fill("tab", 0, 16, -8192); fill("tab", 5904, 5920, -8192); fill("hi", 0, 2, -8192); fill("hi", 560, 562, -8192)
        fill("n8", 0, 544, -8); fill("lwn", 0, 32, 0); fill("lwp", 0, 128, 0)
        iota(A("tf2", 0, 128), [[1, 64], [0, 2]])
        ts(A("bof"), A("bof"), C(1), O.is_equal)
        ts(A("og", 0, 16), A("j0", 0, 16), C(2), O.is_equal)
        ts(A("w1"), A("jr"), 15.0, O.is_equal)
        ts(A("w2"), A("jr"), 14.0, O.is_equal)
        ts(C(13), C(6), 14.0, O.add)
        ts(C(14), C(6), -256.0, O.mult, 256.0, O.add)
        cp(A("bo"), A("bof"))
        tt(A("w2"), A("w2"), A("w1"), O.add)
        ts(A("a1"), A("jr"), C(13), O.is_equal, C(9), O.mult)
        ts(A("a2"), A("w1"), C(14), O.mult)
        ts(A("w256"), A("w2"), 256.0, O.mult)
        ts(A("nid"), IDN, -8192.0, O.mult)
        tt(A("tri"), A("tri"), A("bo"), O.mult)
        ts(A("dmp"), A("dmp"), C(2), O.add)
        tt(A("tri"), A("tri"), A("nid"), O.add)
        ts(A("s16", 16, 36, 18), A("j0", 0, 2), 0.0, O.mult, A("og", 0, 1), O.add)
        ts(C(15), C(7), 37.0, O.mult)
        ts(C(17), C(2), 37.0, O.mult)
        ts(C(16), C(3), 256.0, O.mult, C(15), O.add)
        ts(A("s16"), A("s16"), 16.0, O.mult)
        ts(A("nid"), IDN, -1.0, O.mult)

    def consts_t(t):
        ts(A("ti", 0, 32), A("jb", 128, 160), C(17), O.add, float(t), O.add)
        ts(A("ti", 128, 256), A("jb", 0, 128), C(16), O.add, float(t), O.add)
        ts(A("ti2", 0, 32), A("ti", 0, 32), 511, O.bitwise_and)
        ts(A("ti2", 128, 256), A("ti", 128, 256), 511, O.bitwise_and)
        cp(A("pj"), A("ti2", 0, 32))
        cp(A("jk"), A("ti2", 128, 192))
        ts(A("j5"), A("ti2", 128, 256), 5.0, O.mult)

    def consts_c():
        ts(C(20), C(1), 8.0, O.mult, C(4), O.add)
        ts(C(21), C(6), -1000.0, O.mult, C(20), O.add)
        ts(C(22), C(6), 1000.0, O.mult, -1000.0, O.add)
        ts(A("pm", 0, 128), A("tf2", 0, 128), C(21), O.is_equal)
        ts(C(22), C(22), C(20), O.add)
        ts(A("pm", 128, 256), A("tf2", 0, 128), C(22), O.is_equal)

    def consts_d():
        act(A("b9"), A("b8"), bias=8192.0)
        act(C(18), C(2), bias=-12296.0)
        act(C(19), C(7), bias=-4.0)
        act(A("pm", 256, 512), A("pm", 0, 256), scale=17.0)
        act(A("wc"), A("w1"), scale=241.0)
        act(A("i38"), IDN, scale=3856.0)
        act(A("ik"), A("b8", 0, 256), scale=0.5, bias=C(19))
        act(PB(7, 0, 256), A("b8", 0, 256), bias=C(18))

    def values(j, src):
        for r, s in enumerate(src):
            mm(PB(j % 6, 128 * r, 128 * r + 128), [(s, A("qbd"))])

    def sign(j, dst, n=512):
        if j % 2:
            act(A(dst, 512 * j, 512 * j + n), PB(j % 6, 0, n), AF.Sign)
        else:
            ts(A(dst, 512 * j, 512 * j + n), PB(j % 6, 0, n), 1.0, O.min, -1.0, O.max)

    def gram(dst, cs, last):
        for c in cs:
            s = A(dst, 128 * c, 128 * c + 128)
            mm1(PB(6, 256, 384), s, s, c == 0, c == last)

    def chunks(x, j):
        return [A(x, 2048 * (c // 16) + c % 16, 2048 * (c // 16 + 1), 16) for c in range(4 * j, 4 * j + 4)]

    def share(t, n):
        cn = "cnt%d" % t
        tt(A("dg", 0, n), PB(6, 256, 256 + n), A("idn", 0, n), O.mult)
        red(A(cn, 4 * rank, 4 * rank + 1), A("dg", 0, n), O.add)
        peers = [c for c in cores if c != core]
        near = [c for c in peers if topo.chip(c) == topo.chip(core)]
        far = [c for c in peers if c not in near]
        fe = topo.engines(core, far[0])
        masks = [sum(1 << e for e in topo.engines(core, near[0]) if e not in fe), topo.mask(core, far[0])]
        mine = T[cn][:, 4 * rank:4 * rank + 1]

        def send(q):
            trs = [RemoteDMATransfer(dst_ids=[DstId(rid=topo.addr(c)[0], pnc=topo.addr(c)[1]) for c in cs], dma_engine_mask=m,
                                     remote_sem=T.sem["cn%d" % t], src=mine, dsts=[mine] * len(cs)) for cs, m in zip((near, far), masks)]
            return q.remote_dma_fused(trs, local_sem=T.sem.sent)
        rec("g", send, None, [A(cn, 4 * rank, 4 * rank + 1)])
        ns = [bin(m).count("1") for m in masks]
        sent[0] += sum(ns)
        ops.append({"e": None, "w": [(cn, 4 * k, 4 * k + 1, 1) for k in range(8) if k != rank], "r": [], "dma": None,
                    "tok": ("cn%d" % t, ns[0] * len(near) + ns[1] * len(far))})

    def list_small(nl, early=None):
        w = nl * FW
        scan(A("gx", 1, w + 1), A("keep", 0, w), A("fl", 0, w), 0.0, O.mult, O.add)
        n8, n16 = w // 8, w // 16
        tot = [(A("bo"), A("gx", 256, w, FW))]
        if early:
            mm(PB(7, 288, 288 + nl), tot)
        mm(PB(2, 0, n8), [(win("a1", 2 * a + 1), A("fl", a, w, 8)) for a in range(8)] +
           [(win("w256", 2 * a + 1), A("gx", a, w, 8)) for a in range(8)])
        mm(PB(3, 0, n8), [(win("a2", 2 * a + 1), A("fl", a, w, 8)) for a in range(8)])
        if not early:
            mm(PB(7, 288, 288 + nl), tot)
        mm(PB(4, 256, 256 + n16), [(win("w1", a), A("gx", a, w, 16)) for a in range(16)])
        mm(PB(4, 256 + n16, 256 + 2 * n16), [(win("w1", a), A("gx", a + 1, w + 1, 16)) for a in range(16)] + [(IDN, A("s16", 0, n16))])
        if early:
            early()
        cp(A("ti", 0, n8), PB(2, 0, n8))
        ts(A("ti2", 0, n8), A("ti", 0, n8), 4095, O.bitwise_and)
        tt(A("tf", 0, n8), A("ti2", 0, n8), PB(3, 0, n8), O.add)
        ts(A("ohi", 0, n8), A("tf", 0, n8), -2288.0, O.add, 0.0, O.max)
        ts(A("olo", 0, n8), A("tf", 0, n8), 1808.0, O.add, 5904.0, O.min)

    def list_off(nl):
        n16 = nl * FW // 16
        ts(A("c01", 0, 2 * n16), PB(4, 256, 256 + 2 * n16), -7.5, O.add, 0.0625, O.mult)
        tt(A("tf", 72, 72 + n16), A("c01", 0, n16), A("c01", n16, 2 * n16), O.is_equal)
        tt(A("tf", 112, 112 + n16), A("tf", 72, 72 + n16), A("dmp", 0, n16), O.mult)
        tt(A("tf", 152, 152 + n16), A("tf", 112, 112 + n16), A("c01", 0, n16), O.add)
        cp(A("osc", 0, n16), A("tf", 152, 152 + n16))

    PCS = ((0, 288), (288, 544))

    def list_hi(l):
        for a, b in PCS:
            act(A("hi", 560 * l + 2 + a, 560 * l + 2 + b), IND(A("tab"), A("ohi", 36 * l + a // 16, 36 * l + b // 16)), bias=-16.0)

    def list_lo(l, dst, between):
        for a, b in PCS:
            tt(A("d1", a, b), IND(A("tab"), A("olo", 36 * l + a // 16, 36 * l + b // 16)), A("hi", 560 * l + a, 560 * l + b), O.max)
        scan(A("sc"), A("n8"), A("d1"), -8192.0, O.add, O.max)
        between()
        tt(IND(A(dst), A("osc", 18 * l, 18 * l + 17)), A("sc", 1, 544, 2), A("b8"), O.add)

    consts_a()
    for j in range(6):
        values(j, chunks("xa", j))
    for j in range(4):
        act(A("st", 512 * j, 512 * j + 512), PB(j), AF.Sign)
    act(A("xc", 0, 1024), A("xa", 0, 1024), scale=-1.0, bias=255.0)
    gram("st", range(8), 31); values(6, chunks("xa", 6)); values(7, chunks("xa", 7)); gram("st", range(8, 16), 31)
    for j in range(4, 8):
        sign(j, "st"); gram("st", range(4 * j, 4 * j + 4), 31)
    share(0, 128)
    for k in range(12):
        table(k, (k + 2) % 6)
    consts_b()
    consts_t(0)
    for t in range(3):
        cur, nxt = ("xa", "xb") if t % 2 == 0 else ("xb", "xa")
        own = A(cur, 0, W)
        cn, gs, gl = "cnt%d" % t, "gs%d" % t, "gl%d" % t

        def comp(k):
            act(A("xc", 1024 * k, 1024 * k + 1024), A(cur, 1024 * k, 1024 * k + 1024), scale=-1.0, bias=255.0)

        def nzq(k):
            if t < 2:
                act(A("nz", 1024 * k, 1024 * k + 1024), A("st", 1024 * k, 1024 * k + 1024), AF.Abs)

        if t:
            comp(0); comp(1)
        red(C(24), A(cn, 0, 33, 4), O.add)
        ts(A("kr"), A("og"), C(24), O.mult)
        mm(PB(7, 256, 272), [(A("bof"), A("kr", 0, 16))])
        if t:
            sign(6, "st")
        red(C(25), PB(7, 256, 272), O.min)
        ts(A("r2"), A("kr", 16, 32), C(25), O.is_equal, C(2), O.mult)
        mm(PB(7, 272, 288), [(A("one"), A("rowc")), (A("one"), A("r2"))])
        ts(A("kr", 0, 16), PB(7, 256, 272), C(25), O.is_equal)
        ts(A("osel"), PB(7, 272, 288), C(26), O.add)
        cp(A("ft"), IND(A("st"), A("osel")))
        for bk in (0, 1):
            for h in range(2):
                mm(PB(bk, 128 * h, 128 * h + 128), [(A("ft", 128 * h, 128 * h + 128), IDN)])
        tt(A("kr", 0, 16), A("kr", 0, 16), A("qf"), O.mult)
        red(C(27), A("kr", 0, 16), O.add)
        ts(A("fl", FW, FW + 256), PB(0, 0, 256), 0.0, O.is_lt)
        act(A("fl", 0, 256), PB(1, 0, 256), AF.Relu)
        comp(2)
        list_small(2)
        mm(PB(6, 0, 256), [(A("tri"), A("fl", FW, FW + 256)), (A("bo"), A("gx", FW, FW + 256))])
        ts(A(gs, 512, 576), A("jk"), PB(7, 289, 290), O.is_ge, -32768.0, O.mult)
        list_hi(1); list_hi(0)
        if t == 0:
            consts_c()
        act(A("lo"), IND(A("tab"), A("olo", 0, 34)))
        for k, (a, b) in enumerate(PCS):
            mm(PB(k, 0, b - a), [(IDN, A("hi", a, b)), (IDN, A("lo", a, b))])
        comp(3)
        list_lo(1, "lwn", lambda: list_off(2))
        cp(A("ol", 0, 32), A("lwn", 0, 32))
        act(A("g1", 0, 256), IND(own, A("ol", 0, 16)))
        cp(A("g1", 256, 512), IND(own, A("ol", 16, 32)))
        act(A(gs, 0, 256), IND(A("g1"), A("pj", 0, 16)))
        cp(A(gs, 256, 512), IND(A("g1"), A("pj", 16, 32)))
        pc = cores[rank ^ XS[t]]
        pm_ = topo.mask(core, pc)
        rec("g", lambda q, gs=gs, gl=gl, pc=pc, pm_=pm_, t=t: q.remote_dma(
            T[gl][:], T[gs][:], T.sem["gu%d" % t], T.sem.sent, topo.addr(pc)[1], topo.addr(pc)[0], pm_), None, [A(gs)])
        sent[0] += bin(pm_).count("1")
        ops.append({"e": None, "w": [(gl, 0, GW, 1)], "r": [], "dma": None, "tok": ("gu%d" % t, bin(pm_).count("1"))})
        if t == 0:
            fill("lws", 0, 176, 0); fill("z", W, W + 16, 255); fill("xa", W + ZC, W + ZW, 0); fill("xb", W + ZC, W + ZW, 0)
            consts_d()
        act(A("wq"), A("w1"), scale=C(27))
        act(A("wq2"), A("w2"), scale=C(27))
        if t < 2:
            act(C(28), C(24), AF.Sign, scale=-1.0, bias=C(25))
            act(C(31), A(cn, 32, 33), bias=65536.0)
            act(A("cnt%d" % (t + 1), 32, 33), C(28), scale=65536.0, bias=C(31))
        scan(A("sc", 0, 288), A("n8", 0, 288), PB(0, 0, 288), -16384.0, O.add, O.max)
        scan(A("sc", 288, 544), A("n8", 0, 256), PB(1, 0, 256), A("sc", 287, 288), O.add, O.max)
        tt(IND(A("lwp"), A("osc", 0, 17)), A("sc", 1, 544, 2), A("b9"), O.add)
        cp(A("op"), A("lwp", 0, 128))
        act(A("pp", 0, 512), IND(own, A("op", 0, 32)))
        act(A("pp", 1024, 2048), IND(own, A("op", 64, 128)))
        for s in range(2):
            for k in (1, 0):
                for h in range(2):
                    mm(PB(4 + s, 128 * (1 - k) + h, 128 * (2 - k), 2),
                       [(A("pm", 256 * k + 128 * h, 256 * k + 128 * h + 128), A("lwp", 64 * s, 64 * s + 64))])
        cp(A("pp", 512, 1024), IND(own, A("op", 32, 64)))

        def step(s, wsrc):
            a, b = 128 * s, 128 * s + 128
            tt(A("t", a, b), PB(4 + s, 0, 128), wsrc, O.add)
            ts(A("v", a, b), A("t", a, b), 4095, O.bitwise_and)
            cp(A("off", a, b), A("v", a, b))
            ts(A("w", a, b), A("v", a, b), 5.0, O.mult, 1.0, O.add)
            tt(A("eq", a, b), A("v", a, b), PB(4 + s, 128, 256), O.is_equal)

        nd, hp = 2048 - NA, NA // 2

        def pieces(s, n=1):
            return [(2048 * s + nd + hp * j, 1024 * s + 512 * j, 2 * (s if n else 1) + j) for j in range(2)]

        def gath(s):
            for k0, g0, bk in pieces(s):
                act(A("ga", g0, g0 + hp), IND(own, A("off", k0 // 16, (k0 + hp) // 16)))

        def count(s, a, b):
            mm(PB(4 + s, a, b), [(A("i38"), A("eq", 128 * s + a, 128 * s + b))] +
               [(win("wc", r), A("msk", 2048 * s + 16 * a + r, 2048 * s + 16 * b, 16)) for r in range(16)])

        def phase(s, n, mid=None):
            if n or s:
                gath(s)
            if n:
                act(A("al", 256 * (n + 1) + 128 * s, 256 * (n + 1) + 128 * s + 128), PB(4 + s, 0, 128), AF.Sign)
            for k0, g0, bk in pieces(s, n):
                mm(PB(bk, 0, hp), [(IDN, A("z", k0, k0 + hp)), (IDN, A("ga", g0, g0 + hp))])
            k0 = 2048 * s
            tt(A("msk", k0, k0 + nd), IND(A("xc"), A("off", k0 // 16, (k0 + nd) // 16)), A("z", k0, k0 + nd), O.is_lt)
            for k1, g0, bk in pieces(s, n):
                act(A("msk", k1, k1 + hp), PB(bk, 0, hp), AF.Sigmoid, bias=-65408.0, scale=256.0)
            if mid:
                mid()
            if n == 4:
                if s == 0:
                    for m in range(5):
                        mm1(PB(6, 256, 512), IDN, A("al", 256 * m, 256 * m + 256), m == 0, False)
                mm1(PB(6, 256 + 128 * s, 384 + 128 * s), IDN, A("al", 1280 + 128 * s, 1408 + 128 * s), False, s == 1)
            if n == 4 and s == 1:
                count(s, 0, nd // 16); count(s, nd // 16, 128)
            else:
                count(s, 0, 128)

        def child(qd, b, bk, e):
            for h in range(2):
                g0 = 256 * (h ^ b)
                mm(PB(bk, 256 * h, 256 * h + 256), [(A("nid"), A("pp", 512 * qd + 256 * h, 512 * qd + 256 * h + 256)),
                                                    (A("nid"), A(gl, g0, g0 + 256))])
            dst = A("z", 1024 * qd + b, 1024 * qd + 1024, 2)
            if e == "a":
                act(dst, PB(bk), AF.Relu, bias=255.0)
            else:
                ts(dst, PB(bk), 255.0, O.add, 0.0, O.max)

        def sums(s, n):
            if n == 0:
                mm(PB(6, 256 + 128 * s, 384 + 128 * s), [(win("wq2", 2 * c + 1), A("pp", 1024 * s + c, 1024 * s + 1024, 8)) for c in range(8)])
            if n == 1:
                mm(PB(7, 296 + 32 * s, 328 + 32 * s), [(IDN, A(gl, 512 + 32 * s, 544 + 32 * s))] +
                   [(win("wq", 2 * c + b), A(gl, c + 256 * (s ^ b), 256 + 256 * (s ^ b), 8)) for c in range(8) for b in range(2)])

        step(0, A("j5"))
        gath(0)
        if t == 0:
            comp(1)
        step(1, A("j5"))
        child(0, 0, 0, "v"); child(0, 1, 1, "v"); child(1, 0, 2, "v"); child(1, 1, 3, "v")
        child(2, 0, 0, "a"); child(2, 1, 1, "a")
        phase(0, 0, lambda: (child(3, 0, 0, "v"), child(3, 1, 1, "a")))
        phase(1, 0)
        ts(A("al", 0, 256), A("ik"), PB(7, 288, 289), O.is_lt)
        for n in range(4):
            for s in range(2):
                step(s, A("w", 128 * s, 128 * s + 128))
                phase(s, n + 1, lambda: sums(s, n))
                if n == 2 and s == 0:
                    act(A("nsg"), PB(7, 296, 360), scale=-1.0)
                if n == 2 and s == 1:
                    for k in range(4):
                        tt(A("al", 256 + 64 * k, 320 + 64 * k), PB(6, 256 + 64 * k, 320 + 64 * k), A("nsg"), O.is_ge)
        ts(A("alv"), PB(6, 256, 512), 6.0, O.is_equal)
        tt(A("fl", 0, 128), PB(4, 0, 128), A("alv", 0, 128), O.min)
        nzq(0)
        if t < 2:
            consts_t(t + 1)
        tt(A("fl", 128, 256), PB(5, 0, 128), A("alv", 128, 256), O.min)

        def early():
            ts(C(29), PB(7, 288, 289), 8192.0, O.mult, -float(2 ** 26 + 12288), O.add)
            act(A("tf2"), PB(6, 0, 256), bias=C(29), scale=-8192.0)
        list_small(1, early)
        list_hi(0)
        tt(A("sc", 0, 256), PB(6, 0, 256), A("tf2"), O.min)
        tt(A("nw"), PB(7, 0, 256), A("sc", 0, 256), O.max)
        ts(A("off"), A("nw"), 12288.0, O.add)
        if t < 2:
            act(A("kp"), A("tf2"), AF.Sigmoid, bias=-8192.0, scale=-1.0)
            for h in range(2):
                mm(PB(0, 128 * h, 128 * h + 128), [(A("kp", 128 * h, 128 * h + 128), IDN)])
            nzq(1)
            act(A("kt"), PB(0, 0, 256))
            nzq(2); nzq(3)

        def mid():
            list_off(1)
            if t < 2:
                ts(C(30), PB(7, 288, 289), PB(7, 289, 290), O.min, -12288.0, O.add)
                ts(PB(1, 0, 176), PB(7, 0, 176), C(30), O.is_ge, 4096.0, O.mult)
        list_lo(0, "lws", mid)
        if t < 2:
            tt(A("w", 0, 176), PB(1, 0, 176), A("lws", 0, 176), O.max)
            cp(A("ol", 0, 176), A("w", 0, 176))
            mm(PB(6, 384, 392), [(A("nz", 128 * c, 128 * c + 128), A("kt", 128 * (c // 16) + c % 16, 128 * (c // 16 + 1), 16)) for c in range(32)])
        else:
            cp(A("ol", 0, 176), A("lws", 0, 176))
        for a, b, e in ((0, 512, "v"), (512, 1024, "a"), (1024, 1536, "v"), (1536, 2048, "a"), (2048, 2304, "v"), (2304, ZC, "a")):
            dst, src = A(cur, W + a, W + b), IND(A("z"), A("ol", a // 16, b // 16))
            if e == "a":
                act(dst, src, scale=-1.0, bias=255.0)
            else:
                ts(dst, src, -1.0, O.mult, 255.0, O.add)
        if t < 2:
            for j in range(6):
                values(j, [A(cur, W + 128 * c, W + 128 * c + 128) for c in range(4 * j, min(4 * j + 4, 22))])
            for j in range(6):
                sign(j, "msk", 512 if j < 5 else 256); gram("msk", range(4 * j, min(4 * j + 4, 22)), 21)
            share(t + 1, 136)
        cw = 512 if t == 2 else 1024
        for k in range(W // cw):
            dst, src = A(nxt, cw * k, cw * k + cw), IND(A(cur), A("off", cw // 16 * k, cw // 16 * (k + 1)))
            if k % 2:
                act(dst, src)
            else:
                cp(dst, src)
            if t == 2:
                rec("s", lambda q, k=k, dst=dst: q.dma_start(T.y[:, 512 * k:512 * k + 512], dst[0]), None, [dst], ("sty", 128), "sty")
        if t < 2:
            for j in range(6):
                values(j, chunks(nxt, j))
            sign(0, "st"); sign(1, "st"); values(6, chunks(nxt, 6)); values(7, chunks(nxt, 7))
            for j in range(2, 6):
                sign(j, "st")
            sign(7, "st")
    _emit(g, T, ops, [("sent", sent[0]), ("sty", 128)])
